import numpy as np
import ml_dtypes


def mxq(x, axis, fmt="e4m3"):
    dtype, down = {"e4m3": (ml_dtypes.float8_e4m3fn, 7), "e5m2": (ml_dtypes.float8_e5m2, 14)}[fmt]
    v = np.moveaxis(np.asarray(x, np.float32).astype(ml_dtypes.bfloat16).astype(np.float64), axis, -1)
    blocks = v.reshape(v.shape[:-1] + (-1, 32))
    amax = np.abs(blocks).max(-1, keepdims=True)
    byte = np.maximum(np.where(amax > 0, np.frexp(amax)[1] - 1 + 127, 0) - down, 1)
    scale = np.exp2(byte - 127.0)
    codes = (blocks / scale).astype(np.float32).astype(dtype).astype(np.float64)
    return np.moveaxis((codes * scale).reshape(v.shape), -1, axis)


WIDE = False


def mx_kscale(k):
    if not WIDE:
        return np.ones(k)
    levels = np.array([10, -10, 5, -5, 0])
    if k % 512:
        return np.exp2(np.random.permutation(np.resize(levels, k // 32))).repeat(32)
    a = np.empty((k // 512, 16))
    for p in range(k // 512):
        a[p, :8] = np.random.permutation(np.resize(levels, 8))
        for g in range(8):
            far = levels[np.abs(levels - a[p, g]) >= 10]
            a[p, g + 8] = far[np.random.randint(len(far))]
    return np.exp2(a.ravel()).repeat(32)


def f64(x):
    return np.asarray(x).astype(np.float64)


def striped(idx):
    return np.tile(idx.reshape(-1, 16).T, (8, 1)).astype(np.uint16)


def unstriped(offs):
    return offs[:16].T.reshape(-1).astype(np.int64)


def silu(v):
    return v / (1.0 + np.exp(-np.maximum(v, -700.0)))


K, T, S, H, N = 1024, 1024, 512, 512, 256


def setup_inputs():
    n = np.random.standard_normal
    s = mx_kscale(K)[:, None]
    u = mx_kscale(H)
    return {
        "xT": (n((K, T)) * s).astype(np.float32),
        "w1": (n((K, H)) / np.sqrt(K) / s * u).astype(np.float32),
        "w2": (n((H, N)) / np.sqrt(H) / u[:, None]).astype(np.float32),
        "offs": striped(np.sort(np.random.permutation(T)[:S])),
    }


def reference(xT, w1, w2, offs):
    idx = unstriped(offs)
    xq = mxq(f64(xT)[:, idx], 0, "e4m3")
    h = silu(mxq(f64(w1), 0, "e4m3").T @ xq)
    y = mxq(f64(w2), 0, "e4m3").T @ mxq(h, 0, "e4m3")
    return y

@@ -1,0 +1,169 @@
+from contextlib import ExitStack
+
+import concourse.mybir as mybir
+from concourse.masks import make_identity
+
+K, T, S, H, N = 1024, 1024, 512, 512, 256
+FLOPS = 2 * S * (K * H + H * N)
+
+F32 = mybir.dt.float32
+BF16 = mybir.dt.bfloat16
+U32 = mybir.dt.uint32
+U16 = mybir.dt.uint16
+U8 = mybir.dt.uint8
+FP8X4 = mybir.dt.float8_e4m3fn_x4
+COPY = mybir.ActivationFunctionType.Copy
+SILU = mybir.ActivationFunctionType.Silu
+
+P = 128
+PASSES = K // 512
+G = 128
+GROUPS = S // G
+X_SCALAR = ((256, 288), (704, 512))
+W1_SCALAR = (96, 56)
+WARM = 12
+
+
+def tile_picked_pick_mlp_silu_srt_e_kernel(tc, xT, w1, w2, offs, out):
+    nc = tc.nc
+    with ExitStack() as ctx:
+        keep = ctx.enter_context(tc.tile_pool(name="keep", bufs=1))
+        psum = ctx.enter_context(tc.psum_pool(name="psum", bufs=1))
+
+        x_hbm = xT.rearrange("(s p u e) t -> s u p e t", p=P, u=2, e=2)
+        w1_hbm = w1.rearrange("(s p j) c -> s p j c", p=P, j=4)
+        w2_hbm = w2.rearrange("(p j) c -> p j c", j=4)
+        out_hbm = out.rearrange("(m p) n -> p m n", p=P)
+
+        offsets = keep.tile([P, S // 16], U16, name="offsets")
+        x_raw = [[keep.tile([P, 2, T], F32, name="x_raw%d%d" % (s, u)) for u in range(2)] for s in range(PASSES)]
+        w1_raw = [keep.tile([P, 4, H], F32, name="w1_raw%d" % s) for s in range(PASSES)]
+        w2_raw = keep.tile([P, 4, N], F32, name="w2_raw")
+        nc.sync.dma_start(x_raw[0][0][:], x_hbm[0, 0])
+        nc.sync.dma_start(offsets[:], offs)
+        nc.sync.dma_start(x_raw[0][1][:], x_hbm[0, 1])
+        for u in range(2):
+            nc.sync.dma_start(x_raw[1][u][:], x_hbm[1, u])
+        for s in range(PASSES):
+            nc.sync.dma_start(w1_raw[s][:], w1_hbm[s])
+        nc.sync.dma_start(w2_raw[:], w2_hbm)
+
+        table = keep.tile([P, 1], F32, name="table")
+        nc.vector.memset(table[:], 0.0)
+        nc.scalar.activation(table[:], table[:], SILU)
+        identity = keep.tile([P, P], BF16, name="identity")
+        make_identity(nc, identity[:])
+
+        def codes_and_scales(name, width):
+            codes = keep.tile([P, width], U32, name=name + "_codes", align_bytes=64)
+            scales = keep.tile([P, width], U8, name=name + "_scales", align_bytes=64)
+            return codes, scales
+
+        def quantize(pair, grouped, lo, hi):
+            codes, scales = pair
+            nc.vector.quantize_mx(
+                out=codes[:, lo:hi].bitcast(FP8X4), scales=scales[:, lo:hi], in_=grouped[:, 4 * lo : 4 * hi]
+            )
+
+        def matmul_mx(bank, stationary, cols, moving, toks, start, stop):
+            nc.tensor.matmul_mx(
+                out=bank,
+                lhsT=stationary[0][:, cols].bitcast(FP8X4),
+                lhsT_scale=stationary[1][:, cols],
+                rhs=moving[0][:, toks].bitcast(FP8X4),
+                rhs_scale=moving[1][:, toks],
+                start=start,
+                stop=stop,
+            )
+
+        warm_bank = psum.tile([P, 4, P], BF16, name="warm_bank", tag="y_bank2")
+        spare_bank = psum.tile([P, S], F32, name="spare_bank", tag="y_bank3")
+        h_banks = [psum.tile([P, 4, G], F32, name="h_bank%d" % g) for g in range(GROUPS)]
+
+        x_mx = []
+        for s in range(PASSES):
+            planes = keep.tile([P, 2, S * 2], BF16, name="planes%d" % s, align_bytes=64)
+            for u in range(2):
+                window = keep.tile([P, T * 2], BF16, name="window%d%d" % (s, u), align_bytes=64)
+                pairs = window[:].rearrange("p (t e) -> p t e", e=2)
+                raw = x_raw[s][u][:].rearrange("p e t -> p t e")
+                a = X_SCALAR[s][u]
+                nc.scalar.activation(pairs[:, :a, :], raw[:, :a, :], COPY)
+                nc.vector.tensor_copy(pairs[:, a:, :], raw[:, a:, :])
+                nc.vector.tensor_copy(planes[:, u, :].bitcast(U32), window[:].bitcast(U32).indirect(offsets[:]))
+            picked = keep.tile([P, S * 4], BF16, name="picked%d" % s, align_bytes=64)
+            nc.vector.tensor_copy(
+                picked[:].rearrange("p (n u e) -> p n u e", u=2, e=2), planes[:].rearrange("p u (n e) -> p n u e", e=2)
+            )
+            x_mx.append(codes_and_scales("x%d" % s, S))
+            quantize(x_mx[s], picked, 0, S)
+
+        for i in range(WARM):
+            nc.tensor.transpose(warm_bank[:, i % 4, :], picked[:, P * i : P * (i + 1)], identity[:])
+
+        w1_mx = [codes_and_scales("w1_%d" % s, H) for s in range(PASSES)]
+
+        def first_layer(g, t, s):
+            cols, toks = slice(P * t, P * (t + 1)), slice(G * g, G * (g + 1))
+            matmul_mx(h_banks[g][:, t, :], w1_mx[s], cols, x_mx[s], toks, s == 0, s == PASSES - 1)
+
+        for s in range(PASSES):
+            grouped = keep.tile([P, H * 4], BF16, name="w1_grouped%d" % s, align_bytes=64)
+            dst = grouped[:].rearrange("p (t m j) -> p m j t", t=4, j=4)
+            src = w1_raw[s][:].rearrange("p j (m t) -> p m j t", t=4)
+            a = W1_SCALAR[s]
+            nc.scalar.activation(dst[:, :a, :, :], src[:, :a, :, :], COPY)
+            nc.vector.tensor_copy(dst[:, a:, :, :], src[:, a:, :, :])
+            if s == 0:
+                quantize(w1_mx[s], grouped, 0, H)
+                matmul_mx(spare_bank[:], w1_mx[0], slice(0, P), x_mx[0], slice(0, S), True, True)
+                for g in range(GROUPS):
+                    first_layer(g, 0, 0)
+            else:
+                quantize(w1_mx[s], grouped, 0, H // 2)
+                quantize(w1_mx[s], grouped, H // 2, H)
+
+        y_banks = [psum.tile([P, 2, G], F32, name="y_bank%d" % g, tag="y_bank%d" % g) for g in range(GROUPS)]
+        hidden = [keep.tile([P, G * 4], BF16, name="hidden%d" % g, align_bytes=64) for g in range(GROUPS)]
+        h_mx = [codes_and_scales("h%d" % g, G) for g in range(GROUPS)]
+        results = [keep.tile([P, 2, G], F32, name="result%d" % g) for g in range(GROUPS)]
+        w2_grouped = keep.tile([P, N * 4], BF16, name="w2_grouped", align_bytes=64)
+        w2_mx = codes_and_scales("w2", N)
+
+        def hide(g):
+            first_layer(g, 0, 1)
+            for t in range(1, 4):
+                for s in range(PASSES):
+                    first_layer(g, t, s)
+            nc.scalar.activation(
+                hidden[g][:].rearrange("p (n t) -> p n t", t=4), h_banks[g][:].rearrange("p t n -> p n t"), SILU
+            )
+
+        def second_layer(g):
+            quantize(h_mx[g], hidden[g], 0, G)
+            for m in range(2):
+                matmul_mx(y_banks[g][:, m, :], w2_mx, slice(P * m, P * (m + 1)), h_mx[g], slice(0, G), True, True)
+
+        def store(g):
+            if g == GROUPS - 2:
+                nc.scalar.activation(results[g][:], y_banks[g][:], COPY)
+            else:
+                nc.vector.tensor_copy(results[g][:], y_banks[g][:])
+            nc.sync.dma_start(out_hbm[:, :, G * g : G * (g + 1)], results[g][:])
+
+        hide(0)
+        nc.vector.tensor_copy(
+            w2_grouped[:].rearrange("p (c i j) -> p c j i", i=4, j=4), w2_raw[:].rearrange("p j (c i) -> p c j i", i=4)
+        )
+        quantize(w2_mx, w2_grouped, 0, N)
+        hide(1)
+        hide(2)
+        second_layer(0)
+        hide(3)
+        second_layer(1)
+        store(0)
+        second_layer(2)
+        store(1)
+        second_layer(3)
+        store(2)
+        store(3)

@@ -1,7 +1,6 @@
 from contextlib import ExitStack
 
 import concourse.mybir as mybir
-from concourse.masks import make_identity
 
 K, T, S, H, N = 1024, 1024, 512, 512, 256
 FLOPS = 2 * S * (K * H + H * N)
@@ -19,9 +18,10 @@ P = 128
 PASSES = K // 512
 G = 128
 GROUPS = S // G
-X_SCALAR = ((256, 288), (704, 512))
-W1_SCALAR = (96, 56)
-WARM = 12
+EARLY = T - S + S // 2
+X_SCALAR = ((376, 376), (876, EARLY))
+W1_SCALAR = (104, 72)
+WARM = 2
 
 
 def tile_picked_pick_mlp_silu_srt_e_kernel(tc, xT, w1, w2, offs, out):
@@ -36,23 +36,24 @@ def tile_picked_pick_mlp_silu_srt_e_kernel(tc, xT, w1, w2, offs, out):
         out_hbm = out.rearrange("(m p) n -> p m n", p=P)
 
         offsets = keep.tile([P, S // 16], U16, name="offsets")
-        x_raw = [[keep.tile([P, 2, T], F32, name="x_raw%d%d" % (s, u)) for u in range(2)] for s in range(PASSES)]
+        widths = ((T, T), (T, EARLY))
+        x_raw = [[keep.tile([P, 2, widths[s][u]], F32, name="x_raw%d%d" % (s, u)) for u in range(2)] for s in range(PASSES)]
+        x_late = keep.tile([P, 2, T - EARLY], F32, name="x_late")
         w1_raw = [keep.tile([P, 4, H], F32, name="w1_raw%d" % s) for s in range(PASSES)]
         w2_raw = keep.tile([P, 4, N], F32, name="w2_raw")
         nc.sync.dma_start(x_raw[0][0][:], x_hbm[0, 0])
         nc.sync.dma_start(offsets[:], offs)
         nc.sync.dma_start(x_raw[0][1][:], x_hbm[0, 1])
         for u in range(2):
-            nc.sync.dma_start(x_raw[1][u][:], x_hbm[1, u])
+            nc.sync.dma_start(x_raw[1][u][:], x_hbm[1, u, :, :, : widths[1][u]])
         for s in range(PASSES):
             nc.sync.dma_start(w1_raw[s][:], w1_hbm[s])
+        nc.sync.dma_start(x_late[:], x_hbm[1, 1, :, :, EARLY:])
         nc.sync.dma_start(w2_raw[:], w2_hbm)
 
         table = keep.tile([P, 1], F32, name="table")
         nc.vector.memset(table[:], 0.0)
         nc.scalar.activation(table[:], table[:], SILU)
-        identity = keep.tile([P, P], BF16, name="identity")
-        make_identity(nc, identity[:])
 
         def codes_and_scales(name, width):
             codes = keep.tile([P, width], U32, name=name + "_codes", align_bytes=64)
@@ -76,30 +77,37 @@ def tile_picked_pick_mlp_silu_srt_e_kernel(tc, xT, w1, w2, offs, out):
                 stop=stop,
             )
 
-        warm_bank = psum.tile([P, 4, P], BF16, name="warm_bank", tag="y_bank2")
         spare_bank = psum.tile([P, S], F32, name="spare_bank", tag="y_bank3")
-        h_banks = [psum.tile([P, 4, G], F32, name="h_bank%d" % g) for g in range(GROUPS)]
+        h_banks = [psum.tile([P, 4, G], F32, name="h_bank%d" % g, tag="h_bank%d" % g) for g in range(GROUPS)]
 
-        x_mx = []
+        x_mx = [codes_and_scales("x%d" % s, S) for s in range(PASSES)]
+        planes = [keep.tile([P, 2, S * 2], BF16, name="planes%d" % s, align_bytes=64) for s in range(PASSES)]
+        picked = [keep.tile([P, S * 4], BF16, name="picked%d" % s, align_bytes=64) for s in range(PASSES)]
+
+        def gather(s, u, window, lo, hi):
+            nc.vector.tensor_copy(
+                planes[s][:, u, 2 * lo : 2 * hi].bitcast(U32),
+                window[:, : 2 * (T - S + hi)].bitcast(U32).indirect(offsets[:, lo // 16 : hi // 16]),
+            )
+
+        def weave(s, lo, hi):
+            nc.vector.tensor_copy(
+                picked[s][:, 4 * lo : 4 * hi].rearrange("p (n u e) -> p n u e", u=2, e=2),
+                planes[s][:, :, 2 * lo : 2 * hi].rearrange("p u (n e) -> p n u e", e=2),
+            )
+            quantize(x_mx[s], picked[s], lo, hi)
+
         for s in range(PASSES):
-            planes = keep.tile([P, 2, S * 2], BF16, name="planes%d" % s, align_bytes=64)
             for u in range(2):
                 window = keep.tile([P, T * 2], BF16, name="window%d%d" % (s, u), align_bytes=64)
                 pairs = window[:].rearrange("p (t e) -> p t e", e=2)
                 raw = x_raw[s][u][:].rearrange("p e t -> p t e")
-                a = X_SCALAR[s][u]
+                a, width = X_SCALAR[s][u], widths[s][u]
                 nc.scalar.activation(pairs[:, :a, :], raw[:, :a, :], COPY)
-                nc.vector.tensor_copy(pairs[:, a:, :], raw[:, a:, :])
-                nc.vector.tensor_copy(planes[:, u, :].bitcast(U32), window[:].bitcast(U32).indirect(offsets[:]))
-            picked = keep.tile([P, S * 4], BF16, name="picked%d" % s, align_bytes=64)
-            nc.vector.tensor_copy(
-                picked[:].rearrange("p (n u e) -> p n u e", u=2, e=2), planes[:].rearrange("p u (n e) -> p n u e", e=2)
-            )
-            x_mx.append(codes_and_scales("x%d" % s, S))
-            quantize(x_mx[s], picked, 0, S)
-
-        for i in range(WARM):
-            nc.tensor.transpose(warm_bank[:, i % 4, :], picked[:, P * i : P * (i + 1)], identity[:])
+                if a < width:
+                    nc.vector.tensor_copy(pairs[:, a:width, :], raw[:, a:, :])
+                gather(s, u, window, 0, width - (T - S))
+            weave(s, 0, width - (T - S))
 
         w1_mx = [codes_and_scales("w1_%d" % s, H) for s in range(PASSES)]
 
@@ -113,20 +121,22 @@ def tile_picked_pick_mlp_silu_srt_e_kernel(tc, xT, w1, w2, offs, out):
             src = w1_raw[s][:].rearrange("p j (m t) -> p m j t", t=4)
             a = W1_SCALAR[s]
             nc.scalar.activation(dst[:, :a, :, :], src[:, :a, :, :], COPY)
-            nc.vector.tensor_copy(dst[:, a:, :, :], src[:, a:, :, :])
+            if a < P:
+                nc.vector.tensor_copy(dst[:, a:, :, :], src[:, a:, :, :])
             if s == 0:
                 quantize(w1_mx[s], grouped, 0, H)
-                matmul_mx(spare_bank[:], w1_mx[0], slice(0, P), x_mx[0], slice(0, S), True, True)
+                for i in range(WARM):
+                    matmul_mx(spare_bank[:], w1_mx[0], slice(0, P), x_mx[0], slice(0, S), True, True)
                 for g in range(GROUPS):
                     first_layer(g, 0, 0)
             else:
                 quantize(w1_mx[s], grouped, 0, H // 2)
                 quantize(w1_mx[s], grouped, H // 2, H)
 
-        y_banks = [psum.tile([P, 2, G], F32, name="y_bank%d" % g, tag="y_bank%d" % g) for g in range(GROUPS)]
+        y_banks = [psum.tile([P, 2, G], F32, name="y_bank%d" % g, tag="y_bank%d" % g) for g in range(GROUPS - 1)]
         hidden = [keep.tile([P, G * 4], BF16, name="hidden%d" % g, align_bytes=64) for g in range(GROUPS)]
         h_mx = [codes_and_scales("h%d" % g, G) for g in range(GROUPS)]
-        results = [keep.tile([P, 2, G], F32, name="result%d" % g) for g in range(GROUPS)]
+        results = [keep.tile([P, 2, G], F32, name="result%d" % g) for g in range(GROUPS - 1)]
         w2_grouped = keep.tile([P, N * 4], BF16, name="w2_grouped", align_bytes=64)
         w2_mx = codes_and_scales("w2", N)
 
@@ -145,16 +155,21 @@ def tile_picked_pick_mlp_silu_srt_e_kernel(tc, xT, w1, w2, offs, out):
                 matmul_mx(y_banks[g][:, m, :], w2_mx, slice(P * m, P * (m + 1)), h_mx[g], slice(0, G), True, True)
 
         def store(g):
-            if g == GROUPS - 2:
+            if g > 0:
                 nc.scalar.activation(results[g][:], y_banks[g][:], COPY)
             else:
                 nc.vector.tensor_copy(results[g][:], y_banks[g][:])
             nc.sync.dma_start(out_hbm[:, :, G * g : G * (g + 1)], results[g][:])
 
-        hide(0)
-        nc.vector.tensor_copy(
-            w2_grouped[:].rearrange("p (c i j) -> p c j i", i=4, j=4), w2_raw[:].rearrange("p j (c i) -> p c j i", i=4)
+        nc.scalar.activation(pairs[:, EARLY:, :], x_late[:].rearrange("p e t -> p t e"), COPY)
+        gather(1, 1, window, S // 2, S)
+        weave(1, S // 2, S)
+        nc.scalar.activation(
+            w2_grouped[:].rearrange("p (c i j) -> p c j i", i=4, j=4),
+            w2_raw[:].rearrange("p j (c i) -> p c j i", i=4),
+            COPY,
         )
+        hide(0)
         quantize(w2_mx, w2_grouped, 0, N)
         hide(1)
         hide(2)
@@ -164,6 +179,16 @@ def tile_picked_pick_mlp_silu_srt_e_kernel(tc, xT, w1, w2, offs, out):
         store(0)
         second_layer(2)
         store(1)
-        second_layer(3)
+        last = GROUPS - 1
+        quantize(h_mx[last], hidden[last], 0, G)
         store(2)
-        store(3)
+        for m, tag in enumerate(("y_bank3", "h_bank0")):
+            bank = psum.tile([P, G], F32, name="last_bank%d" % m, tag=tag)
+            result = keep.tile([P, G], F32, name="last_result%d" % m)
+            matmul_mx(bank[:], w2_mx, slice(P * m, P * (m + 1)), h_mx[last], slice(0, G), True, True)
+            if m == 0:
+                nc.vector.tensor_copy(result[:], bank[:])
+                nc.sync.dma_start(out_hbm[:, m, G * last :], result[:])
+            else:
+                nc.scalar.activation(result[:], bank[:], COPY)
+                nc.scalar.dma_start(out_hbm[:, m, G * last :], result[:])

@@ -19,8 +19,9 @@ PASSES = K // 512
 G = 128
 GROUPS = S // G
 EARLY = T - S + S // 2
-X_SCALAR = ((376, 376), (876, EARLY))
-W1_SCALAR = (104, 72)
+X_SCALAR = ((320, 320), (704, 528))
+W1_SCALAR = (80, 52)
+W2_SCALAR = 40
 WARM = 2
 
 
@@ -163,13 +164,13 @@ def tile_picked_pick_mlp_silu_srt_e_kernel(tc, xT, w1, w2, offs, out):
 
         nc.scalar.activation(pairs[:, EARLY:, :], x_late[:].rearrange("p e t -> p t e"), COPY)
         gather(1, 1, window, S // 2, S)
-        weave(1, S // 2, S)
-        nc.scalar.activation(
-            w2_grouped[:].rearrange("p (c i j) -> p c j i", i=4, j=4),
-            w2_raw[:].rearrange("p j (c i) -> p c j i", i=4),
-            COPY,
-        )
+        for g in range(GROUPS // 2, GROUPS):
+            weave(1, G * g, G * (g + 1))
+        w2_dst = w2_grouped[:].rearrange("p (c i j) -> p c j i", i=4, j=4)
+        w2_src = w2_raw[:].rearrange("p j (c i) -> p c j i", i=4)
+        nc.scalar.activation(w2_dst[:, :W2_SCALAR], w2_src[:, :W2_SCALAR], COPY)
         hide(0)
+        nc.vector.tensor_copy(w2_dst[:, W2_SCALAR:], w2_src[:, W2_SCALAR:])
         quantize(w2_mx, w2_grouped, 0, N)
         hide(1)
         hide(2)

@@ -8,6 +8,7 @@ FLOPS = 2 * S * (K * H + H * N)
 F32 = mybir.dt.float32
 BF16 = mybir.dt.bfloat16
 U32 = mybir.dt.uint32
+I32 = mybir.dt.int32
 U16 = mybir.dt.uint16
 U8 = mybir.dt.uint8
 FP8X4 = mybir.dt.float8_e4m3fn_x4
@@ -19,9 +20,9 @@ PASSES = K // 512
 G = 128
 GROUPS = S // G
 EARLY = T - S + S // 2
-X_SCALAR = ((320, 320), (704, 528))
-W1_SCALAR = (80, 52)
-W2_SCALAR = 40
+X_SCALAR = ((320, 320), (0, EARLY))
+W1_SCALAR = (96, 66)
+W2_SCALAR = 48
 WARM = 2
 
 
@@ -91,12 +92,11 @@ def tile_picked_pick_mlp_silu_srt_e_kernel(tc, xT, w1, w2, offs, out):
                 window[:, : 2 * (T - S + hi)].bitcast(U32).indirect(offsets[:, lo // 16 : hi // 16]),
             )
 
-        def weave(s, lo, hi):
-            nc.vector.tensor_copy(
-                picked[s][:, 4 * lo : 4 * hi].rearrange("p (n u e) -> p n u e", u=2, e=2),
-                planes[s][:, :, 2 * lo : 2 * hi].rearrange("p u (n e) -> p n u e", e=2),
+        def weave(engine_copy, dtype, s, lo, hi):
+            engine_copy(
+                picked[s][:, 4 * lo : 4 * hi].bitcast(dtype).rearrange("p (n u) -> p n u", u=2),
+                planes[s][:, :, 2 * lo : 2 * hi].bitcast(dtype).rearrange("p u n -> p n u"),
             )
-            quantize(x_mx[s], picked[s], lo, hi)
 
         for s in range(PASSES):
             for u in range(2):
@@ -104,11 +104,19 @@ def tile_picked_pick_mlp_silu_srt_e_kernel(tc, xT, w1, w2, offs, out):
                 pairs = window[:].rearrange("p (t e) -> p t e", e=2)
                 raw = x_raw[s][u][:].rearrange("p e t -> p t e")
                 a, width = X_SCALAR[s][u], widths[s][u]
-                nc.scalar.activation(pairs[:, :a, :], raw[:, :a, :], COPY)
+                if a > 0:
+                    nc.scalar.activation(pairs[:, :a, :], raw[:, :a, :], COPY)
                 if a < width:
                     nc.vector.tensor_copy(pairs[:, a:width, :], raw[:, a:, :])
                 gather(s, u, window, 0, width - (T - S))
-            weave(s, 0, width - (T - S))
+            if s == 0:
+                weave(nc.scalar.copy, U32, s, 0, S)
+            else:
+                weave(nc.vector.tensor_copy, I32, s, 0, S // 2)
+            quantize(x_mx[s], picked[s], 0, width - (T - S))
+
+        for i in range(WARM):
+            matmul_mx(spare_bank[:], x_mx[1], slice(0, P), x_mx[0], slice(0, S), True, True)
 
         w1_mx = [codes_and_scales("w1_%d" % s, H) for s in range(PASSES)]
 
@@ -126,18 +134,17 @@ def tile_picked_pick_mlp_silu_srt_e_kernel(tc, xT, w1, w2, offs, out):
                 nc.vector.tensor_copy(dst[:, a:, :, :], src[:, a:, :, :])
             if s == 0:
                 quantize(w1_mx[s], grouped, 0, H)
-                for i in range(WARM):
-                    matmul_mx(spare_bank[:], w1_mx[0], slice(0, P), x_mx[0], slice(0, S), True, True)
                 for g in range(GROUPS):
                     first_layer(g, 0, 0)
             else:
                 quantize(w1_mx[s], grouped, 0, H // 2)
                 quantize(w1_mx[s], grouped, H // 2, H)
 
-        y_banks = [psum.tile([P, 2, G], F32, name="y_bank%d" % g, tag="y_bank%d" % g) for g in range(GROUPS - 1)]
-        hidden = [keep.tile([P, G * 4], BF16, name="hidden%d" % g, align_bytes=64) for g in range(GROUPS)]
-        h_mx = [codes_and_scales("h%d" % g, G) for g in range(GROUPS)]
-        results = [keep.tile([P, 2, G], F32, name="result%d" % g) for g in range(GROUPS - 1)]
+        pieces = ((0, 2 * G), (2 * G, 3 * G))
+        y_banks = [psum.tile([P, 2, hi - lo], F32, name="y_bank%d" % i) for i, (lo, hi) in enumerate(pieces)]
+        hidden = keep.tile([P, S * 4], BF16, name="hidden", align_bytes=64)
+        h_mx = codes_and_scales("h", S)
+        results = [keep.tile([P, 2, hi - lo], F32, name="result%d" % i) for i, (lo, hi) in enumerate(pieces)]
         w2_grouped = keep.tile([P, N * 4], BF16, name="w2_grouped", align_bytes=64)
         w2_mx = codes_and_scales("w2", N)
 
@@ -147,25 +154,28 @@ def tile_picked_pick_mlp_silu_srt_e_kernel(tc, xT, w1, w2, offs, out):
                 for s in range(PASSES):
                     first_layer(g, t, s)
             nc.scalar.activation(
-                hidden[g][:].rearrange("p (n t) -> p n t", t=4), h_banks[g][:].rearrange("p t n -> p n t"), SILU
+                hidden[:, 4 * G * g : 4 * G * (g + 1)].rearrange("p (n t) -> p n t", t=4), h_banks[g][:].rearrange("p t n -> p n t"), SILU
             )
 
-        def second_layer(g):
-            quantize(h_mx[g], hidden[g], 0, G)
+        def second_layer(i):
+            lo, hi = pieces[i]
+            quantize(h_mx, hidden, lo, hi)
             for m in range(2):
-                matmul_mx(y_banks[g][:, m, :], w2_mx, slice(P * m, P * (m + 1)), h_mx[g], slice(0, G), True, True)
+                matmul_mx(y_banks[i][:, m, :], w2_mx, slice(P * m, P * (m + 1)), h_mx, slice(lo, hi), True, True)
 
-        def store(g):
-            if g > 0:
-                nc.scalar.activation(results[g][:], y_banks[g][:], COPY)
+        def store(i):
+            lo, hi = pieces[i]
+            if i > 0:
+                nc.scalar.activation(results[i][:], y_banks[i][:], COPY)
             else:
-                nc.vector.tensor_copy(results[g][:], y_banks[g][:])
-            nc.sync.dma_start(out_hbm[:, :, G * g : G * (g + 1)], results[g][:])
+                nc.vector.tensor_copy(results[i][:], y_banks[i][:])
+            nc.sync.dma_start(out_hbm[:, :, lo:hi], results[i][:])
 
         nc.scalar.activation(pairs[:, EARLY:, :], x_late[:].rearrange("p e t -> p t e"), COPY)
         gather(1, 1, window, S // 2, S)
+        weave(nc.vector.tensor_copy, I32, 1, S // 2, S)
         for g in range(GROUPS // 2, GROUPS):
-            weave(1, G * g, G * (g + 1))
+            quantize(x_mx[1], picked[1], G * g, G * (g + 1))
         w2_dst = w2_grouped[:].rearrange("p (c i j) -> p c j i", i=4, j=4)
         w2_src = w2_raw[:].rearrange("p j (c i) -> p c j i", i=4)
         nc.scalar.activation(w2_dst[:, :W2_SCALAR], w2_src[:, :W2_SCALAR], COPY)
@@ -178,15 +188,13 @@ def tile_picked_pick_mlp_silu_srt_e_kernel(tc, xT, w1, w2, offs, out):
         hide(3)
         second_layer(1)
         store(0)
-        second_layer(2)
-        store(1)
         last = GROUPS - 1
-        quantize(h_mx[last], hidden[last], 0, G)
-        store(2)
+        quantize(h_mx, hidden, G * last, S)
+        store(1)
         for m, tag in enumerate(("y_bank3", "h_bank0")):
             bank = psum.tile([P, G], F32, name="last_bank%d" % m, tag=tag)
             result = keep.tile([P, G], F32, name="last_result%d" % m)
-            matmul_mx(bank[:], w2_mx, slice(P * m, P * (m + 1)), h_mx[last], slice(0, G), True, True)
+            matmul_mx(bank[:], w2_mx, slice(P * m, P * (m + 1)), h_mx, slice(G * last, S), True, True)
             if m == 0:
                 nc.vector.tensor_copy(result[:], bank[:])
                 nc.sync.dma_start(out_hbm[:, m, G * last :], result[:])

@@ -94,20 +94,20 @@ def tile_picked_pick_mlp_silu_srt_e_kernel(tc, xT, w1, w2, offs, out):
 
         def weave(engine_copy, dtype, s, lo, hi):
             engine_copy(
-                picked[s][:, 4 * lo : 4 * hi].bitcast(dtype).rearrange("p (n u) -> p n u", u=2),
-                planes[s][:, :, 2 * lo : 2 * hi].bitcast(dtype).rearrange("p u n -> p n u"),
+                picked[s][:, 4 * lo : 4 * hi].bitcast(dtype).rearrange("p (c i u) -> p c u i", i=2, u=2),
+                planes[s][:, :, 2 * lo : 2 * hi].bitcast(dtype).rearrange("p u (c i) -> p c u i", i=2),
             )
 
         for s in range(PASSES):
             for u in range(2):
                 window = keep.tile([P, T * 2], BF16, name="window%d%d" % (s, u), align_bytes=64)
-                pairs = window[:].rearrange("p (t e) -> p t e", e=2)
-                raw = x_raw[s][u][:].rearrange("p e t -> p t e")
+                pairs = window[:].rearrange("p (c i e) -> p c e i", i=4, e=2)
+                raw = x_raw[s][u][:].rearrange("p e (c i) -> p c e i", i=4)
                 a, width = X_SCALAR[s][u], widths[s][u]
                 if a > 0:
-                    nc.scalar.activation(pairs[:, :a, :], raw[:, :a, :], COPY)
+                    nc.scalar.activation(pairs[:, : a // 4], raw[:, : a // 4], COPY)
                 if a < width:
-                    nc.vector.tensor_copy(pairs[:, a:width, :], raw[:, a:, :])
+                    nc.vector.tensor_copy(pairs[:, a // 4 : width // 4], raw[:, a // 4 :])
                 gather(s, u, window, 0, width - (T - S))
             if s == 0:
                 weave(nc.scalar.copy, U32, s, 0, S)
@@ -171,7 +171,7 @@ def tile_picked_pick_mlp_silu_srt_e_kernel(tc, xT, w1, w2, offs, out):
                 nc.vector.tensor_copy(results[i][:], y_banks[i][:])
             nc.sync.dma_start(out_hbm[:, :, lo:hi], results[i][:])
 
-        nc.scalar.activation(pairs[:, EARLY:, :], x_late[:].rearrange("p e t -> p t e"), COPY)
+        nc.scalar.activation(pairs[:, EARLY // 4 :], x_late[:].rearrange("p e (c i) -> p c e i", i=4), COPY)
         gather(1, 1, window, S // 2, S)
         weave(nc.vector.tensor_copy, I32, 1, S // 2, S)
         for g in range(GROUPS // 2, GROUPS):

@@ -8,7 +8,6 @@ FLOPS = 2 * S * (K * H + H * N)
 F32 = mybir.dt.float32
 BF16 = mybir.dt.bfloat16
 U32 = mybir.dt.uint32
-I32 = mybir.dt.int32
 U16 = mybir.dt.uint16
 U8 = mybir.dt.uint8
 FP8X4 = mybir.dt.float8_e4m3fn_x4
@@ -19,11 +18,8 @@ P = 128
 PASSES = K // 512
 G = 128
 GROUPS = S // G
-EARLY = T - S + S // 2
-X_SCALAR = ((320, 320), (0, EARLY))
-W1_SCALAR = (96, 66)
-W2_SCALAR = 48
-WARM = 2
+WEAVE_VECTOR = 352
+W1_SCALAR = (128, 84)
 
 
 def tile_picked_pick_mlp_silu_srt_e_kernel(tc, xT, w1, w2, offs, out):
@@ -32,33 +28,34 @@ def tile_picked_pick_mlp_silu_srt_e_kernel(tc, xT, w1, w2, offs, out):
         keep = ctx.enter_context(tc.tile_pool(name="keep", bufs=1))
         psum = ctx.enter_context(tc.psum_pool(name="psum", bufs=1))
 
-        x_hbm = xT.rearrange("(s p u e) t -> s u p e t", p=P, u=2, e=2)
+        x_hbm = xT.rearrange("(s p j) t -> s p j t", p=P, j=4)
         w1_hbm = w1.rearrange("(s p j) c -> s p j c", p=P, j=4)
         w2_hbm = w2.rearrange("(p j) c -> p j c", j=4)
         out_hbm = out.rearrange("(m p) n -> p m n", p=P)
 
         offsets = keep.tile([P, S // 16], U16, name="offsets")
-        widths = ((T, T), (T, EARLY))
-        x_raw = [[keep.tile([P, 2, widths[s][u]], F32, name="x_raw%d%d" % (s, u)) for u in range(2)] for s in range(PASSES)]
-        x_late = keep.tile([P, 2, T - EARLY], F32, name="x_late")
-        w1_raw = [keep.tile([P, 4, H], F32, name="w1_raw%d" % s) for s in range(PASSES)]
+        loads = ((0, 0, 2), (0, 2, 4), (1, 0, 2), (1, 2, 3), (1, 3, 4))
+        rows = {}
+        w1_raw = [keep.tile([P, 4, H], F32, name="w1_raw%d" % s, tag="w1_raw%d" % s, align_bytes=64) for s in range(PASSES)]
         w2_raw = keep.tile([P, 4, N], F32, name="w2_raw")
-        nc.sync.dma_start(x_raw[0][0][:], x_hbm[0, 0])
-        nc.sync.dma_start(offsets[:], offs)
-        nc.sync.dma_start(x_raw[0][1][:], x_hbm[0, 1])
-        for u in range(2):
-            nc.sync.dma_start(x_raw[1][u][:], x_hbm[1, u, :, :, : widths[1][u]])
-        for s in range(PASSES):
-            nc.sync.dma_start(w1_raw[s][:], w1_hbm[s])
-        nc.sync.dma_start(x_late[:], x_hbm[1, 1, :, :, EARLY:])
+        for i, (s, lo, hi) in enumerate(loads):
+            raw = keep.tile([P, hi - lo, T], F32, name="x_raw%d" % i)
+            if i == len(loads) - 1:
+                nc.sync.dma_start(w1_raw[0][:], w1_hbm[0])
+            nc.sync.dma_start(raw[:], x_hbm[s, :, lo:hi, :])
+            if i == 0:
+                nc.sync.dma_start(offsets[:], offs)
+            for j in range(lo, hi):
+                rows[(s, j)] = raw[:, j - lo, :]
+        nc.sync.dma_start(w1_raw[1][:], w1_hbm[1])
         nc.sync.dma_start(w2_raw[:], w2_hbm)
 
         table = keep.tile([P, 1], F32, name="table")
         nc.vector.memset(table[:], 0.0)
         nc.scalar.activation(table[:], table[:], SILU)
 
-        def codes_and_scales(name, width):
-            codes = keep.tile([P, width], U32, name=name + "_codes", align_bytes=64)
+        def codes_and_scales(name, width, tag=None):
+            codes = keep.tile([P, width], U32, name=name + "_codes", tag=tag or name + "_codes", align_bytes=64)
             scales = keep.tile([P, width], U8, name=name + "_scales", align_bytes=64)
             return codes, scales
 
@@ -79,125 +76,119 @@ def tile_picked_pick_mlp_silu_srt_e_kernel(tc, xT, w1, w2, offs, out):
                 stop=stop,
             )
 
-        spare_bank = psum.tile([P, S], F32, name="spare_bank", tag="y_bank3")
+        def scalar_copy(dst, src):
+            nc.scalar.activation(dst, src, COPY)
+
         h_banks = [psum.tile([P, 4, G], F32, name="h_bank%d" % g, tag="h_bank%d" % g) for g in range(GROUPS)]
 
-        x_mx = [codes_and_scales("x%d" % s, S) for s in range(PASSES)]
-        planes = [keep.tile([P, 2, S * 2], BF16, name="planes%d" % s, align_bytes=64) for s in range(PASSES)]
+        x_mx = {(0, 0): codes_and_scales("x0", S), (1, 0): codes_and_scales("x1_lower", S // 2)}
+        planes = [keep.tile([P, 4, S], F32, name="planes%d" % s) for s in range(PASSES)]
         picked = [keep.tile([P, S * 4], BF16, name="picked%d" % s, align_bytes=64) for s in range(PASSES)]
 
-        def gather(s, u, window, lo, hi):
-            nc.vector.tensor_copy(
-                planes[s][:, u, 2 * lo : 2 * hi].bitcast(U32),
-                window[:, : 2 * (T - S + hi)].bitcast(U32).indirect(offsets[:, lo // 16 : hi // 16]),
+        def gather(copy, s, j, lo, hi):
+            copy(planes[s][:, j, lo:hi], rows[(s, j)].indirect(offsets[:, lo // 16 : hi // 16]))
+
+        def weave(copy, s, lo, hi):
+            copy(
+                picked[s][:, 4 * lo : 4 * hi].rearrange("p (c i j) -> p c j i", i=4, j=4),
+                planes[s][:, :, lo:hi].rearrange("p j (c i) -> p c j i", i=4),
             )
-
-        def weave(engine_copy, dtype, s, lo, hi):
-            engine_copy(
-                picked[s][:, 4 * lo : 4 * hi].bitcast(dtype).rearrange("p (c i u) -> p c u i", i=2, u=2),
-                planes[s][:, :, 2 * lo : 2 * hi].bitcast(dtype).rearrange("p u (c i) -> p c u i", i=2),
-            )
-
-        for s in range(PASSES):
-            for u in range(2):
-                window = keep.tile([P, T * 2], BF16, name="window%d%d" % (s, u), align_bytes=64)
-                pairs = window[:].rearrange("p (c i e) -> p c e i", i=4, e=2)
-                raw = x_raw[s][u][:].rearrange("p e (c i) -> p c e i", i=4)
-                a, width = X_SCALAR[s][u], widths[s][u]
-                if a > 0:
-                    nc.scalar.activation(pairs[:, : a // 4], raw[:, : a // 4], COPY)
-                if a < width:
-                    nc.vector.tensor_copy(pairs[:, a // 4 : width // 4], raw[:, a // 4 :])
-                gather(s, u, window, 0, width - (T - S))
-            if s == 0:
-                weave(nc.scalar.copy, U32, s, 0, S)
-            else:
-                weave(nc.vector.tensor_copy, I32, s, 0, S // 2)
-            quantize(x_mx[s], picked[s], 0, width - (T - S))
-
-        for i in range(WARM):
-            matmul_mx(spare_bank[:], x_mx[1], slice(0, P), x_mx[0], slice(0, S), True, True)
 
         w1_mx = [codes_and_scales("w1_%d" % s, H) for s in range(PASSES)]
+        w1_grouped = [keep.tile([P, H * 4], BF16, name="w1_grouped%d" % s, align_bytes=64) for s in range(PASSES)]
 
         def first_layer(g, t, s):
-            cols, toks = slice(P * t, P * (t + 1)), slice(G * g, G * (g + 1))
-            matmul_mx(h_banks[g][:, t, :], w1_mx[s], cols, x_mx[s], toks, s == 0, s == PASSES - 1)
+            part, first = ((s, 1), g - 2) if s == 1 and g >= 2 else ((s, 0), g)
+            cols, toks = slice(P * t, P * (t + 1)), slice(G * first, G * (first + 1))
+            matmul_mx(h_banks[g][:, t, :], w1_mx[s], cols, x_mx[part], toks, s == 0 and t == 0, s == PASSES - 1 and t == 3)
 
-        for s in range(PASSES):
-            grouped = keep.tile([P, H * 4], BF16, name="w1_grouped%d" % s, align_bytes=64)
-            dst = grouped[:].rearrange("p (t m j) -> p m j t", t=4, j=4)
+        def round_w1(s):
+            dst = w1_grouped[s][:].rearrange("p (t m j) -> p m j t", t=4, j=4)
             src = w1_raw[s][:].rearrange("p j (m t) -> p m j t", t=4)
             a = W1_SCALAR[s]
-            nc.scalar.activation(dst[:, :a, :, :], src[:, :a, :, :], COPY)
+            nc.vector.tensor_copy(dst[:, :, :, :2], src[:, :, :, :2])
+            scalar_copy(dst[:, :a, :, 2:], src[:, :a, :, 2:])
             if a < P:
-                nc.vector.tensor_copy(dst[:, a:, :, :], src[:, a:, :, :])
-            if s == 0:
-                quantize(w1_mx[s], grouped, 0, H)
-                for g in range(GROUPS):
-                    first_layer(g, 0, 0)
-            else:
-                quantize(w1_mx[s], grouped, 0, H // 2)
-                quantize(w1_mx[s], grouped, H // 2, H)
+                nc.vector.tensor_copy(dst[:, a:, :, 2:], src[:, a:, :, 2:])
 
-        pieces = ((0, 2 * G), (2 * G, 3 * G))
-        y_banks = [psum.tile([P, 2, hi - lo], F32, name="y_bank%d" % i) for i, (lo, hi) in enumerate(pieces)]
+        def first_pass(half):
+            quantize(w1_mx[0], w1_grouped[0], half * H // 2, (half + 1) * H // 2)
+            for g in range(GROUPS):
+                for t in range(2 * half, 2 * half + 2):
+                    first_layer(g, t, 0)
+
+        gather(scalar_copy, 0, 0, 0, S)
+        gather(nc.vector.tensor_copy, 0, 1, 0, S)
+        gather(scalar_copy, 0, 2, 0, S)
+        gather(nc.vector.tensor_copy, 0, 3, 0, S)
+        weave(nc.vector.tensor_copy, 0, 0, WEAVE_VECTOR)
+        weave(scalar_copy, 0, WEAVE_VECTOR, S)
+        quantize(x_mx[(0, 0)], picked[0], 0, S)
+        gather(scalar_copy, 1, 0, 0, S)
+        gather(nc.vector.tensor_copy, 1, 1, 0, S)
+        gather(scalar_copy, 1, 2, 0, S)
+        round_w1(0)
+        first_pass(0)
+        gather(nc.vector.tensor_copy, 1, 3, 0, S // 2)
+        gather(scalar_copy, 1, 3, S // 2, S)
+        first_pass(1)
+        weave(nc.vector.tensor_copy, 1, 0, S // 2)
+        weave(scalar_copy, 1, S // 2, S)
+        quantize(x_mx[(1, 0)], picked[1], 0, S // 2)
+        round_w1(1)
+        quantize(w1_mx[1], w1_grouped[1], 0, H // 2)
+        quantize(w1_mx[1], w1_grouped[1], H // 2, H)
+        x_mx[(1, 1)] = codes_and_scales("x1_upper", S // 2, tag="w1_raw1")
+        quantize(x_mx[(1, 1)], picked[1][:, 2 * S :], 0, S // 2)
+
+        last = GROUPS - 1
+        y_banks = [psum.tile([P, 2, G], F32, name="y_bank%d" % g) for g in range(last)]
         hidden = keep.tile([P, S * 4], BF16, name="hidden", align_bytes=64)
         h_mx = codes_and_scales("h", S)
-        results = [keep.tile([P, 2, hi - lo], F32, name="result%d" % i) for i, (lo, hi) in enumerate(pieces)]
+        result = keep.tile([P, 2, G * last], F32, name="result")
         w2_grouped = keep.tile([P, N * 4], BF16, name="w2_grouped", align_bytes=64)
         w2_mx = codes_and_scales("w2", N)
 
         def hide(g):
-            first_layer(g, 0, 1)
-            for t in range(1, 4):
-                for s in range(PASSES):
-                    first_layer(g, t, s)
+            for t in range(4):
+                first_layer(g, t, 1)
             nc.scalar.activation(
                 hidden[:, 4 * G * g : 4 * G * (g + 1)].rearrange("p (n t) -> p n t", t=4), h_banks[g][:].rearrange("p t n -> p n t"), SILU
             )
 
-        def second_layer(i):
-            lo, hi = pieces[i]
-            quantize(h_mx, hidden, lo, hi)
+        def second_layer(g):
+            quantize(h_mx, hidden, G * g, G * (g + 1))
             for m in range(2):
-                matmul_mx(y_banks[i][:, m, :], w2_mx, slice(P * m, P * (m + 1)), h_mx, slice(lo, hi), True, True)
+                matmul_mx(y_banks[g][:, m, :], w2_mx, slice(P * m, P * (m + 1)), h_mx, slice(G * g, G * (g + 1)), True, True)
 
-        def store(i):
-            lo, hi = pieces[i]
-            if i > 0:
-                nc.scalar.activation(results[i][:], y_banks[i][:], COPY)
-            else:
-                nc.vector.tensor_copy(results[i][:], y_banks[i][:])
-            nc.sync.dma_start(out_hbm[:, :, lo:hi], results[i][:])
+        def copy_out(g):
+            nc.vector.tensor_copy(result[:, :, G * g : G * (g + 1)], y_banks[g][:])
 
-        nc.scalar.activation(pairs[:, EARLY // 4 :], x_late[:].rearrange("p e (c i) -> p c e i", i=4), COPY)
-        gather(1, 1, window, S // 2, S)
-        weave(nc.vector.tensor_copy, I32, 1, S // 2, S)
-        for g in range(GROUPS // 2, GROUPS):
-            quantize(x_mx[1], picked[1], G * g, G * (g + 1))
-        w2_dst = w2_grouped[:].rearrange("p (c i j) -> p c j i", i=4, j=4)
-        w2_src = w2_raw[:].rearrange("p j (c i) -> p c j i", i=4)
-        nc.scalar.activation(w2_dst[:, :W2_SCALAR], w2_src[:, :W2_SCALAR], COPY)
-        hide(0)
-        nc.vector.tensor_copy(w2_dst[:, W2_SCALAR:], w2_src[:, W2_SCALAR:])
+        def store(lo, hi):
+            nc.sync.dma_start(out_hbm[:, :, G * lo : G * hi], result[:, :, G * lo : G * hi])
+
+        for g in range(GROUPS):
+            hide(g)
+        nc.vector.tensor_copy(
+            w2_grouped[:].rearrange("p (c i j) -> p c j i", i=4, j=4), w2_raw[:].rearrange("p j (c i) -> p c j i", i=4)
+        )
         quantize(w2_mx, w2_grouped, 0, N)
-        hide(1)
-        hide(2)
         second_layer(0)
-        hide(3)
         second_layer(1)
-        store(0)
-        last = GROUPS - 1
+        copy_out(0)
+        second_layer(2)
+        copy_out(1)
+        store(0, 2)
         quantize(h_mx, hidden, G * last, S)
-        store(1)
-        for m, tag in enumerate(("y_bank3", "h_bank0")):
+        copy_out(2)
+        store(2, 3)
+        for m, tag in enumerate(("last_bank", "h_bank0")):
             bank = psum.tile([P, G], F32, name="last_bank%d" % m, tag=tag)
-            result = keep.tile([P, G], F32, name="last_result%d" % m)
+            tail = keep.tile([P, G], F32, name="last_result%d" % m)
             matmul_mx(bank[:], w2_mx, slice(P * m, P * (m + 1)), h_mx, slice(G * last, S), True, True)
             if m == 0:
-                nc.vector.tensor_copy(result[:], bank[:])
-                nc.sync.dma_start(out_hbm[:, m, G * last :], result[:])
+                nc.vector.tensor_copy(tail[:], bank[:])
+                nc.sync.dma_start(out_hbm[:, m, G * last :], tail[:])
             else:
-                nc.scalar.activation(result[:], bank[:], COPY)
-                nc.scalar.dma_start(out_hbm[:, m, G * last :], result[:])
+                scalar_copy(tail[:], bank[:])
+                nc.scalar.dma_start(out_hbm[:, m, G * last :], tail[:])

@@ -39,8 +39,8 @@ def tile_picked_pick_mlp_silu_srt_e_kernel(tc, xT, w1, w2, offs, out):
         w1_raw = [keep.tile([P, 4, H], F32, name="w1_raw%d" % s, tag="w1_raw%d" % s, align_bytes=64) for s in range(PASSES)]
         w2_raw = keep.tile([P, 4, N], F32, name="w2_raw")
         for i, (s, lo, hi) in enumerate(loads):
-            raw = keep.tile([P, hi - lo, T], F32, name="x_raw%d" % i)
-            if i == len(loads) - 1:
+            raw = keep.tile([P, hi - lo, T], F32, name="x_raw%d" % i, tag="x_raw%d" % i, align_bytes=64)
+            if i == len(loads) - 2:
                 nc.sync.dma_start(w1_raw[0][:], w1_hbm[0])
             nc.sync.dma_start(raw[:], x_hbm[s, :, lo:hi, :])
             if i == 0:
@@ -94,13 +94,13 @@ def tile_picked_pick_mlp_silu_srt_e_kernel(tc, xT, w1, w2, offs, out):
                 planes[s][:, :, lo:hi].rearrange("p j (c i) -> p c j i", i=4),
             )
 
-        w1_mx = [codes_and_scales("w1_%d" % s, H) for s in range(PASSES)]
+        w1_mx = {}
         w1_grouped = [keep.tile([P, H * 4], BF16, name="w1_grouped%d" % s, align_bytes=64) for s in range(PASSES)]
 
         def first_layer(g, t, s):
             part, first = ((s, 1), g - 2) if s == 1 and g >= 2 else ((s, 0), g)
-            cols, toks = slice(P * t, P * (t + 1)), slice(G * first, G * (first + 1))
-            matmul_mx(h_banks[g][:, t, :], w1_mx[s], cols, x_mx[part], toks, s == 0 and t == 0, s == PASSES - 1 and t == 3)
+            cols, toks = slice(P * (t % 2), P * (t % 2 + 1)), slice(G * first, G * (first + 1))
+            matmul_mx(h_banks[g][:, t, :], w1_mx[(s, t // 2)], cols, x_mx[part], toks, s == 0 and t == 0, s == PASSES - 1 and t == 3)
 
         def round_w1(s):
             dst = w1_grouped[s][:].rearrange("p (t m j) -> p m j t", t=4, j=4)
@@ -111,8 +111,12 @@ def tile_picked_pick_mlp_silu_srt_e_kernel(tc, xT, w1, w2, offs, out):
             if a < P:
                 nc.vector.tensor_copy(dst[:, a:, :, 2:], src[:, a:, :, 2:])
 
-        def first_pass(half):
-            quantize(w1_mx[0], w1_grouped[0], half * H // 2, (half + 1) * H // 2)
+        def quantize_w1(s, half, tag=None):
+            w1_mx[(s, half)] = codes_and_scales("w1_%d%d" % (s, half), H // 2, tag=tag)
+            quantize(w1_mx[(s, half)], w1_grouped[s][:, 2 * H * half :], 0, H // 2)
+
+        def first_pass(half, tag=None):
+            quantize_w1(0, half, tag)
             for g in range(GROUPS):
                 for t in range(2 * half, 2 * half + 2):
                     first_layer(g, t, 0)
@@ -126,18 +130,21 @@ def tile_picked_pick_mlp_silu_srt_e_kernel(tc, xT, w1, w2, offs, out):
         quantize(x_mx[(0, 0)], picked[0], 0, S)
         gather(scalar_copy, 1, 0, 0, S)
         gather(nc.vector.tensor_copy, 1, 1, 0, S)
-        gather(scalar_copy, 1, 2, 0, S)
         round_w1(0)
-        first_pass(0)
-        gather(nc.vector.tensor_copy, 1, 3, 0, S // 2)
+        gather(nc.vector.tensor_copy, 1, 2, 0, S // 2)
+        gather(scalar_copy, 1, 2, S // 2, S)
+        first_pass(0, tag="x_raw3")
+        for g in range(2):
+            gather(nc.vector.tensor_copy, 1, 3, G * g, G * (g + 1))
         gather(scalar_copy, 1, 3, S // 2, S)
-        first_pass(1)
-        weave(nc.vector.tensor_copy, 1, 0, S // 2)
+        for g in range(2):
+            weave(nc.vector.tensor_copy, 1, G * g, G * (g + 1))
         weave(scalar_copy, 1, S // 2, S)
+        first_pass(1, tag="x_raw4")
         quantize(x_mx[(1, 0)], picked[1], 0, S // 2)
         round_w1(1)
-        quantize(w1_mx[1], w1_grouped[1], 0, H // 2)
-        quantize(w1_mx[1], w1_grouped[1], H // 2, H)
+        quantize_w1(1, 0)
+        quantize_w1(1, 1)
         x_mx[(1, 1)] = codes_and_scales("x1_upper", S // 2, tag="w1_raw1")
         quantize(x_mx[(1, 1)], picked[1][:, 2 * S :], 0, S // 2)
 
@@ -161,8 +168,8 @@ def tile_picked_pick_mlp_silu_srt_e_kernel(tc, xT, w1, w2, offs, out):
             for m in range(2):
                 matmul_mx(y_banks[g][:, m, :], w2_mx, slice(P * m, P * (m + 1)), h_mx, slice(G * g, G * (g + 1)), True, True)
 
-        def copy_out(g):
-            nc.vector.tensor_copy(result[:, :, G * g : G * (g + 1)], y_banks[g][:])
+        def copy_out(copy, g):
+            copy(result[:, :, G * g : G * (g + 1)], y_banks[g][:])
 
         def store(lo, hi):
             nc.sync.dma_start(out_hbm[:, :, G * lo : G * hi], result[:, :, G * lo : G * hi])
@@ -175,12 +182,12 @@ def tile_picked_pick_mlp_silu_srt_e_kernel(tc, xT, w1, w2, offs, out):
         quantize(w2_mx, w2_grouped, 0, N)
         second_layer(0)
         second_layer(1)
-        copy_out(0)
+        copy_out(nc.vector.tensor_copy, 0)
         second_layer(2)
-        copy_out(1)
+        copy_out(nc.vector.tensor_copy, 1)
         store(0, 2)
         quantize(h_mx, hidden, G * last, S)
-        copy_out(2)
+        copy_out(scalar_copy, 2)
         store(2, 3)
         for m, tag in enumerate(("last_bank", "h_bank0")):
             bank = psum.tile([P, G], F32, name="last_bank%d" % m, tag=tag)

@@ -152,7 +152,7 @@ def tile_picked_pick_mlp_silu_srt_e_kernel(tc, xT, w1, w2, offs, out):
         y_banks = [psum.tile([P, 2, G], F32, name="y_bank%d" % g) for g in range(last)]
         hidden = keep.tile([P, S * 4], BF16, name="hidden", align_bytes=64)
         h_mx = codes_and_scales("h", S)
-        result = keep.tile([P, 2, G * last], F32, name="result")
+        result = keep.tile([P, 2, S], F32, name="result")
         w2_grouped = keep.tile([P, N * 4], BF16, name="w2_grouped", align_bytes=64)
         w2_mx = codes_and_scales("w2", N)
 
@@ -191,11 +191,7 @@ def tile_picked_pick_mlp_silu_srt_e_kernel(tc, xT, w1, w2, offs, out):
         store(2, 3)
         for m, tag in enumerate(("last_bank", "h_bank0")):
             bank = psum.tile([P, G], F32, name="last_bank%d" % m, tag=tag)
-            tail = keep.tile([P, G], F32, name="last_result%d" % m)
             matmul_mx(bank[:], w2_mx, slice(P * m, P * (m + 1)), h_mx, slice(G * last, S), True, True)
-            if m == 0:
-                nc.vector.tensor_copy(tail[:], bank[:])
-                nc.sync.dma_start(out_hbm[:, m, G * last :], tail[:])
-            else:
-                scalar_copy(tail[:], bank[:])
-                nc.scalar.dma_start(out_hbm[:, m, G * last :], tail[:])
+            copy = nc.vector.tensor_copy if m == 0 else scalar_copy
+            copy(result[:, m, G * last :], bank[:])
+        store(last, GROUPS)

@@ -15,11 +15,11 @@ COPY = mybir.ActivationFunctionType.Copy
 SILU = mybir.ActivationFunctionType.Silu
 
 P = 128
-PASSES = K // 512
 G = 128
 GROUPS = S // G
+HALF = S // 2
 WEAVE_VECTOR = 352
-W1_SCALAR = (128, 84)
+W1_VECTOR = 80
 
 
 def tile_picked_pick_mlp_silu_srt_e_kernel(tc, xT, w1, w2, offs, out):
@@ -34,20 +34,20 @@ def tile_picked_pick_mlp_silu_srt_e_kernel(tc, xT, w1, w2, offs, out):
         out_hbm = out.rearrange("(m p) n -> p m n", p=P)
 
         offsets = keep.tile([P, S // 16], U16, name="offsets")
-        loads = ((0, 0, 2), (0, 2, 4), (1, 0, 2), (1, 2, 3), (1, 3, 4))
-        rows = {}
-        w1_raw = [keep.tile([P, 4, H], F32, name="w1_raw%d" % s, tag="w1_raw%d" % s, align_bytes=64) for s in range(PASSES)]
-        w2_raw = keep.tile([P, 4, N], F32, name="w2_raw")
-        for i, (s, lo, hi) in enumerate(loads):
-            raw = keep.tile([P, hi - lo, T], F32, name="x_raw%d" % i, tag="x_raw%d" % i, align_bytes=64)
-            if i == len(loads) - 2:
-                nc.sync.dma_start(w1_raw[0][:], w1_hbm[0])
-            nc.sync.dma_start(raw[:], x_hbm[s, :, lo:hi, :])
-            if i == 0:
-                nc.sync.dma_start(offsets[:], offs)
-            for j in range(lo, hi):
-                rows[(s, j)] = raw[:, j - lo, :]
+        pair_raw = [keep.tile([P, 2, T], F32, name="pair_raw%d" % u) for u in range(2)]
+        row_raw = [keep.tile([P, T], F32, name="row_raw%d" % j) for j in range(2)]
+        last_raw = [keep.tile([P, T], F32, name="last_raw%d" % j, tag="last_raw%d" % j, align_bytes=64) for j in range(2)]
+        w1_raw = [keep.tile([P, 4, H], F32, name="w1_raw%d" % s, tag="w1_raw%d" % s, align_bytes=64) for s in range(2)]
+        w2_raw = keep.tile([P, 4, N], F32, name="w2_raw", tag="w2_raw", align_bytes=64)
+        nc.sync.dma_start(pair_raw[0][:], x_hbm[0, :, 0:2, :])
+        nc.sync.dma_start(offsets[:], offs)
+        nc.sync.dma_start(pair_raw[1][:], x_hbm[0, :, 2:4, :])
         nc.sync.dma_start(w1_raw[1][:], w1_hbm[1])
+        nc.sync.dma_start(w1_raw[0][:], w1_hbm[0])
+        for j in range(2):
+            nc.sync.dma_start(row_raw[j][:], x_hbm[1, :, j, :])
+        for j in range(2):
+            nc.sync.dma_start(last_raw[j][:], x_hbm[1, :, 2 + j, :])
         nc.sync.dma_start(w2_raw[:], w2_hbm)
 
         table = keep.tile([P, 1], F32, name="table")
@@ -59,11 +59,9 @@ def tile_picked_pick_mlp_silu_srt_e_kernel(tc, xT, w1, w2, offs, out):
             scales = keep.tile([P, width], U8, name=name + "_scales", align_bytes=64)
             return codes, scales
 
-        def quantize(pair, grouped, lo, hi):
+        def quantize(pair, lo, hi, grouped):
             codes, scales = pair
-            nc.vector.quantize_mx(
-                out=codes[:, lo:hi].bitcast(FP8X4), scales=scales[:, lo:hi], in_=grouped[:, 4 * lo : 4 * hi]
-            )
+            nc.vector.quantize_mx(out=codes[:, lo:hi].bitcast(FP8X4), scales=scales[:, lo:hi], in_=grouped)
 
         def matmul_mx(bank, stationary, cols, moving, toks, start, stop):
             nc.tensor.matmul_mx(
@@ -79,81 +77,89 @@ def tile_picked_pick_mlp_silu_srt_e_kernel(tc, xT, w1, w2, offs, out):
         def scalar_copy(dst, src):
             nc.scalar.activation(dst, src, COPY)
 
-        h_banks = [psum.tile([P, 4, G], F32, name="h_bank%d" % g, tag="h_bank%d" % g) for g in range(GROUPS)]
+        def planes(name, rows, lo, hi):
+            return keep.tile([P, rows, hi - lo], F32, name=name), lo
 
-        x_mx = {(0, 0): codes_and_scales("x0", S), (1, 0): codes_and_scales("x1_lower", S // 2)}
-        planes = [keep.tile([P, 4, S], F32, name="planes%d" % s) for s in range(PASSES)]
-        picked = [keep.tile([P, S * 4], BF16, name="picked%d" % s, align_bytes=64) for s in range(PASSES)]
+        def gather(copy, target, j, window, lo, hi):
+            tile, first = target
+            copy(tile[:, j, lo - first : hi - first], window.indirect(offsets[:, lo // 16 : hi // 16]))
 
-        def gather(copy, s, j, lo, hi):
-            copy(planes[s][:, j, lo:hi], rows[(s, j)].indirect(offsets[:, lo // 16 : hi // 16]))
-
-        def weave(copy, s, lo, hi):
+        def weave(copy, s, source, lo, hi, slots):
+            tile, first = source
             copy(
-                picked[s][:, 4 * lo : 4 * hi].rearrange("p (c i j) -> p c j i", i=4, j=4),
-                planes[s][:, :, lo:hi].rearrange("p j (c i) -> p c j i", i=4),
+                picked[s][:, 4 * lo : 4 * hi].rearrange("p (c i j) -> p c j i", i=4, j=4)[:, :, slots, :],
+                tile[:, :, lo - first : hi - first].rearrange("p j (c i) -> p c j i", i=4),
             )
 
+        h_banks = [psum.tile([P, 4, G], F32, name="h_bank%d" % g, tag="h_bank%d" % g) for g in range(GROUPS)]
+        x_mx = [codes_and_scales("x%d" % s, S) for s in range(2)]
+        picked = [keep.tile([P, S * 4], BF16, name="picked%d" % s, align_bytes=64) for s in range(2)]
+        w1_grouped = [keep.tile([P, H * 4], BF16, name="w1_grouped%d" % s, align_bytes=64) for s in range(2)]
         w1_mx = {}
-        w1_grouped = [keep.tile([P, H * 4], BF16, name="w1_grouped%d" % s, align_bytes=64) for s in range(PASSES)]
-
-        def first_layer(g, t, s):
-            part, first = ((s, 1), g - 2) if s == 1 and g >= 2 else ((s, 0), g)
-            cols, toks = slice(P * (t % 2), P * (t % 2 + 1)), slice(G * first, G * (first + 1))
-            matmul_mx(h_banks[g][:, t, :], w1_mx[(s, t // 2)], cols, x_mx[part], toks, s == 0 and t == 0, s == PASSES - 1 and t == 3)
 
         def round_w1(s):
             dst = w1_grouped[s][:].rearrange("p (t m j) -> p m j t", t=4, j=4)
             src = w1_raw[s][:].rearrange("p j (m t) -> p m j t", t=4)
-            a = W1_SCALAR[s]
-            nc.vector.tensor_copy(dst[:, :, :, :2], src[:, :, :, :2])
-            scalar_copy(dst[:, :a, :, 2:], src[:, :a, :, 2:])
-            if a < P:
-                nc.vector.tensor_copy(dst[:, a:, :, 2:], src[:, a:, :, 2:])
+            nc.vector.tensor_copy(dst[:, :W1_VECTOR], src[:, :W1_VECTOR])
+            scalar_copy(dst[:, W1_VECTOR:], src[:, W1_VECTOR:])
 
-        def quantize_w1(s, half, tag=None):
-            w1_mx[(s, half)] = codes_and_scales("w1_%d%d" % (s, half), H // 2, tag=tag)
-            quantize(w1_mx[(s, half)], w1_grouped[s][:, 2 * H * half :], 0, H // 2)
+        def quantize_w1(s):
+            w1_mx[s] = codes_and_scales("w1_%d" % s, H)
+            quantize(w1_mx[s], 0, H, w1_grouped[s][:])
 
-        def first_pass(half, tag=None):
-            quantize_w1(0, half, tag)
-            for g in range(GROUPS):
-                for t in range(2 * half, 2 * half + 2):
-                    first_layer(g, t, 0)
+        def first_layer(g, t, s):
+            cols, toks = slice(P * t, P * (t + 1)), slice(G * g, G * (g + 1))
+            matmul_mx(h_banks[g][:, t, :], w1_mx[s], cols, x_mx[s], toks, s == 0 and t == 0, s == 1 and t == 3)
 
-        gather(scalar_copy, 0, 0, 0, S)
-        gather(nc.vector.tensor_copy, 0, 1, 0, S)
-        gather(scalar_copy, 0, 2, 0, S)
-        gather(nc.vector.tensor_copy, 0, 3, 0, S)
-        weave(nc.vector.tensor_copy, 0, 0, WEAVE_VECTOR)
-        weave(scalar_copy, 0, WEAVE_VECTOR, S)
-        quantize(x_mx[(0, 0)], picked[0], 0, S)
-        gather(scalar_copy, 1, 0, 0, S)
-        gather(nc.vector.tensor_copy, 1, 1, 0, S)
-        round_w1(0)
-        gather(nc.vector.tensor_copy, 1, 2, 0, S // 2)
-        gather(scalar_copy, 1, 2, S // 2, S)
-        first_pass(0, tag="x_raw3")
-        for g in range(2):
-            gather(nc.vector.tensor_copy, 1, 3, G * g, G * (g + 1))
-        gather(scalar_copy, 1, 3, S // 2, S)
-        for g in range(2):
-            weave(nc.vector.tensor_copy, 1, G * g, G * (g + 1))
-        weave(scalar_copy, 1, S // 2, S)
-        first_pass(1, tag="x_raw4")
-        quantize(x_mx[(1, 0)], picked[1], 0, S // 2)
+        def quantize_x(lo, hi):
+            quantize(x_mx[1], lo, hi, picked[1][:, 4 * lo : 4 * hi])
+
+        vector_copy = nc.vector.tensor_copy
+        lower, upper = slice(0, 2), slice(2, 4)
+        planes0 = planes("planes0", 4, 0, S)
+        early = planes("early", 2, 0, S)
+        late = planes("late", 2, HALF, S)
+        for u in range(2):
+            gather(scalar_copy, planes0, 2 * u, pair_raw[u][:, 0, :], 0, S)
+            gather(vector_copy, planes0, 2 * u + 1, pair_raw[u][:, 1, :], 0, S)
+        weave(vector_copy, 0, planes0, 0, WEAVE_VECTOR, slice(0, 4))
+        weave(scalar_copy, 0, planes0, WEAVE_VECTOR, S, slice(0, 4))
+        quantize(x_mx[0], 0, S, picked[0][:])
         round_w1(1)
-        quantize_w1(1, 0)
-        quantize_w1(1, 1)
-        x_mx[(1, 1)] = codes_and_scales("x1_upper", S // 2, tag="w1_raw1")
-        quantize(x_mx[(1, 1)], picked[1][:, 2 * S :], 0, S // 2)
+        quantize_w1(1)
+        round_w1(0)
+        quantize_w1(0)
+        for g in range(GROUPS):
+            for t in range(4):
+                first_layer(g, t, 0)
+        def gather_woven(copy, j, g):
+            copy(
+                picked[1][:, 4 * G * g + 2 + j : 4 * G * (g + 1) : 4],
+                last_raw[j][:].indirect(offsets[:, G * g // 16 : G * (g + 1) // 16]),
+            )
+
+        gather(scalar_copy, early, 0, row_raw[0][:], 0, S)
+        gather(vector_copy, early, 1, row_raw[1][:], 0, HALF)
+        gather(scalar_copy, early, 1, row_raw[1][:], HALF, S)
+        weave(vector_copy, 1, early, 0, S, lower)
+        for j in range(2):
+            gather_woven(vector_copy, j, 0)
+            gather_woven(scalar_copy, j, 1)
+            for lo, hi in ((HALF, S),) if j == 0 else ((HALF, S - G), (S - G, S)):
+                gather(scalar_copy, late, j, last_raw[j][:], lo, hi)
+        for g in range(2):
+            quantize_x(G * g, G * (g + 1))
+        for g in range(2, GROUPS):
+            weave(vector_copy, 1, late, G * g, G * (g + 1), upper)
+        for g in range(2, GROUPS):
+            quantize_x(G * g, G * (g + 1))
 
         last = GROUPS - 1
         y_banks = [psum.tile([P, 2, G], F32, name="y_bank%d" % g) for g in range(last)]
-        hidden = keep.tile([P, S * 4], BF16, name="hidden", align_bytes=64)
-        h_mx = codes_and_scales("h", S)
+        hidden = keep.tile([P, S * 4], BF16, name="hidden", tag="last_raw1", align_bytes=64)
+        h_mx = {}
         result = keep.tile([P, 2, S], F32, name="result")
-        w2_grouped = keep.tile([P, N * 4], BF16, name="w2_grouped", align_bytes=64)
+        w2_grouped = keep.tile([P, N * 4], BF16, name="w2_grouped", tag="w2_grouped", align_bytes=64)
         w2_mx = codes_and_scales("w2", N)
 
         def hide(g):
@@ -163,10 +169,14 @@ def tile_picked_pick_mlp_silu_srt_e_kernel(tc, xT, w1, w2, offs, out):
                 hidden[:, 4 * G * g : 4 * G * (g + 1)].rearrange("p (n t) -> p n t", t=4), h_banks[g][:].rearrange("p t n -> p n t"), SILU
             )
 
+        def quantize_h(g):
+            h_mx[g] = codes_and_scales("h%d" % g, G, tag={0: "w2_raw", 1: "w2_grouped", 3: "w2_raw"}.get(g))
+            quantize(h_mx[g], 0, G, hidden[:, 4 * G * g : 4 * G * (g + 1)])
+
         def second_layer(g):
-            quantize(h_mx, hidden, G * g, G * (g + 1))
+            quantize_h(g)
             for m in range(2):
-                matmul_mx(y_banks[g][:, m, :], w2_mx, slice(P * m, P * (m + 1)), h_mx, slice(G * g, G * (g + 1)), True, True)
+                matmul_mx(y_banks[g][:, m, :], w2_mx, slice(P * m, P * (m + 1)), h_mx[g], slice(0, G), True, True)
 
         def copy_out(copy, g):
             copy(result[:, :, G * g : G * (g + 1)], y_banks[g][:])
@@ -179,19 +189,18 @@ def tile_picked_pick_mlp_silu_srt_e_kernel(tc, xT, w1, w2, offs, out):
         nc.vector.tensor_copy(
             w2_grouped[:].rearrange("p (c i j) -> p c j i", i=4, j=4), w2_raw[:].rearrange("p j (c i) -> p c j i", i=4)
         )
-        quantize(w2_mx, w2_grouped, 0, N)
-        second_layer(0)
-        second_layer(1)
+        quantize(w2_mx, 0, N, w2_grouped[:])
+        for g in range(last):
+            second_layer(g)
         copy_out(nc.vector.tensor_copy, 0)
-        second_layer(2)
-        copy_out(nc.vector.tensor_copy, 1)
-        store(0, 2)
-        quantize(h_mx, hidden, G * last, S)
+        store(0, 1)
+        quantize_h(last)
+        copy_out(scalar_copy, 1)
         copy_out(scalar_copy, 2)
-        store(2, 3)
+        store(1, 3)
         for m, tag in enumerate(("last_bank", "h_bank0")):
             bank = psum.tile([P, G], F32, name="last_bank%d" % m, tag=tag)
-            matmul_mx(bank[:], w2_mx, slice(P * m, P * (m + 1)), h_mx, slice(G * last, S), True, True)
+            matmul_mx(bank[:], w2_mx, slice(P * m, P * (m + 1)), h_mx[last], slice(0, G), True, True)
             copy = nc.vector.tensor_copy if m == 0 else scalar_copy
             copy(result[:, m, G * last :], bank[:])
         store(last, GROUPS)

from contextlib import ExitStack

import concourse.mybir as mybir

K, T, S, H, N = 1024, 1024, 512, 512, 256
FLOPS = 2 * S * (K * H + H * N)

F32 = mybir.dt.float32
BF16 = mybir.dt.bfloat16
U32 = mybir.dt.uint32
U16 = mybir.dt.uint16
U8 = mybir.dt.uint8
FP8X4 = mybir.dt.float8_e4m3fn_x4
COPY = mybir.ActivationFunctionType.Copy
SILU = mybir.ActivationFunctionType.Silu

P = 128
G = 128
GROUPS = S // G
HALF = S // 2
WEAVE_VECTOR = 352
W1_VECTOR = 80


def tile_picked_pick_mlp_silu_srt_e_kernel(tc, xT, w1, w2, offs, out):
    nc = tc.nc
    with ExitStack() as ctx:
        keep = ctx.enter_context(tc.tile_pool(name="keep", bufs=1))
        psum = ctx.enter_context(tc.psum_pool(name="psum", bufs=1))

        x_hbm = xT.rearrange("(s p j) t -> s p j t", p=P, j=4)
        w1_hbm = w1.rearrange("(s p j) c -> s p j c", p=P, j=4)
        w2_hbm = w2.rearrange("(p j) c -> p j c", j=4)
        out_hbm = out.rearrange("(m p) n -> p m n", p=P)

        offsets = keep.tile([P, S // 16], U16, name="offsets")
        pair_raw = [keep.tile([P, 2, T], F32, name="pair_raw%d" % u) for u in range(2)]
        row_raw = [keep.tile([P, T], F32, name="row_raw%d" % j) for j in range(2)]
        last_raw = [keep.tile([P, T], F32, name="last_raw%d" % j, tag="last_raw%d" % j, align_bytes=64) for j in range(2)]
        w1_raw = [keep.tile([P, 4, H], F32, name="w1_raw%d" % s, tag="w1_raw%d" % s, align_bytes=64) for s in range(2)]
        w2_raw = keep.tile([P, 4, N], F32, name="w2_raw", tag="w2_raw", align_bytes=64)
        nc.sync.dma_start(pair_raw[0][:], x_hbm[0, :, 0:2, :])
        nc.sync.dma_start(offsets[:], offs)
        nc.sync.dma_start(pair_raw[1][:], x_hbm[0, :, 2:4, :])
        nc.sync.dma_start(w1_raw[1][:], w1_hbm[1])
        nc.sync.dma_start(w1_raw[0][:], w1_hbm[0])
        for j in range(2):
            nc.sync.dma_start(row_raw[j][:], x_hbm[1, :, j, :])
        for j in range(2):
            nc.sync.dma_start(last_raw[j][:], x_hbm[1, :, 2 + j, :])
        nc.sync.dma_start(w2_raw[:], w2_hbm)

        table = keep.tile([P, 1], F32, name="table")
        nc.vector.memset(table[:], 0.0)
        nc.scalar.activation(table[:], table[:], SILU)

        def codes_and_scales(name, width, tag=None):
            codes = keep.tile([P, width], U32, name=name + "_codes", tag=tag or name + "_codes", align_bytes=64)
            scales = keep.tile([P, width], U8, name=name + "_scales", align_bytes=64)
            return codes, scales

        def quantize(pair, lo, hi, grouped):
            codes, scales = pair
            nc.vector.quantize_mx(out=codes[:, lo:hi].bitcast(FP8X4), scales=scales[:, lo:hi], in_=grouped)

        def matmul_mx(bank, stationary, cols, moving, toks, start, stop):
            nc.tensor.matmul_mx(
                out=bank,
                lhsT=stationary[0][:, cols].bitcast(FP8X4),
                lhsT_scale=stationary[1][:, cols],
                rhs=moving[0][:, toks].bitcast(FP8X4),
                rhs_scale=moving[1][:, toks],
                start=start,
                stop=stop,
            )

        def scalar_copy(dst, src):
            nc.scalar.activation(dst, src, COPY)

        def planes(name, rows, lo, hi):
            return keep.tile([P, rows, hi - lo], F32, name=name), lo

        def gather(copy, target, j, window, lo, hi):
            tile, first = target
            copy(tile[:, j, lo - first : hi - first], window.indirect(offsets[:, lo // 16 : hi // 16]))

        def weave(copy, s, source, lo, hi, slots):
            tile, first = source
            copy(
                picked[s][:, 4 * lo : 4 * hi].rearrange("p (c i j) -> p c j i", i=4, j=4)[:, :, slots, :],
                tile[:, :, lo - first : hi - first].rearrange("p j (c i) -> p c j i", i=4),
            )

        h_banks = [psum.tile([P, 4, G], F32, name="h_bank%d" % g, tag="h_bank%d" % g) for g in range(GROUPS)]
        x_mx = [codes_and_scales("x%d" % s, S) for s in range(2)]
        picked = [keep.tile([P, S * 4], BF16, name="picked%d" % s, align_bytes=64) for s in range(2)]
        w1_grouped = [keep.tile([P, H * 4], BF16, name="w1_grouped%d" % s, align_bytes=64) for s in range(2)]
        w1_mx = {}

        def round_w1(s):
            dst = w1_grouped[s][:].rearrange("p (t m j) -> p m j t", t=4, j=4)
            src = w1_raw[s][:].rearrange("p j (m t) -> p m j t", t=4)
            nc.vector.tensor_copy(dst[:, :W1_VECTOR], src[:, :W1_VECTOR])
            scalar_copy(dst[:, W1_VECTOR:], src[:, W1_VECTOR:])

        def quantize_w1(s):
            w1_mx[s] = codes_and_scales("w1_%d" % s, H)
            quantize(w1_mx[s], 0, H, w1_grouped[s][:])

        def first_layer(g, t, s):
            cols, toks = slice(P * t, P * (t + 1)), slice(G * g, G * (g + 1))
            matmul_mx(h_banks[g][:, t, :], w1_mx[s], cols, x_mx[s], toks, s == 0 and t == 0, s == 1 and t == 3)

        def quantize_x(lo, hi):
            quantize(x_mx[1], lo, hi, picked[1][:, 4 * lo : 4 * hi])

        vector_copy = nc.vector.tensor_copy
        lower, upper = slice(0, 2), slice(2, 4)
        planes0 = planes("planes0", 4, 0, S)
        early = planes("early", 2, 0, S)
        late = planes("late", 2, HALF, S)
        for u in range(2):
            gather(scalar_copy, planes0, 2 * u, pair_raw[u][:, 0, :], 0, S)
            gather(vector_copy, planes0, 2 * u + 1, pair_raw[u][:, 1, :], 0, S)
        weave(vector_copy, 0, planes0, 0, WEAVE_VECTOR, slice(0, 4))
        weave(scalar_copy, 0, planes0, WEAVE_VECTOR, S, slice(0, 4))
        quantize(x_mx[0], 0, S, picked[0][:])
        round_w1(1)
        quantize_w1(1)
        round_w1(0)
        quantize_w1(0)
        for g in range(GROUPS):
            for t in range(4):
                first_layer(g, t, 0)
        def gather_woven(copy, j, g):
            copy(
                picked[1][:, 4 * G * g + 2 + j : 4 * G * (g + 1) : 4],
                last_raw[j][:].indirect(offsets[:, G * g // 16 : G * (g + 1) // 16]),
            )

        gather(scalar_copy, early, 0, row_raw[0][:], 0, S)
        gather(vector_copy, early, 1, row_raw[1][:], 0, HALF)
        gather(scalar_copy, early, 1, row_raw[1][:], HALF, S)
        weave(vector_copy, 1, early, 0, S, lower)
        for j in range(2):
            gather_woven(vector_copy, j, 0)
            gather_woven(scalar_copy, j, 1)
            for lo, hi in ((HALF, S),) if j == 0 else ((HALF, S - G), (S - G, S)):
                gather(scalar_copy, late, j, last_raw[j][:], lo, hi)
        for g in range(2):
            quantize_x(G * g, G * (g + 1))
        for g in range(2, GROUPS):
            weave(vector_copy, 1, late, G * g, G * (g + 1), upper)
        for g in range(2, GROUPS):
            quantize_x(G * g, G * (g + 1))

        last = GROUPS - 1
        y_banks = [psum.tile([P, 2, G], F32, name="y_bank%d" % g) for g in range(last)]
        hidden = keep.tile([P, S * 4], BF16, name="hidden", tag="last_raw1", align_bytes=64)
        h_mx = {}
        result = keep.tile([P, 2, S], F32, name="result")
        w2_grouped = keep.tile([P, N * 4], BF16, name="w2_grouped", tag="w2_grouped", align_bytes=64)
        w2_mx = codes_and_scales("w2", N)

        def hide(g):
            for t in range(4):
                first_layer(g, t, 1)
            nc.scalar.activation(
                hidden[:, 4 * G * g : 4 * G * (g + 1)].rearrange("p (n t) -> p n t", t=4), h_banks[g][:].rearrange("p t n -> p n t"), SILU
            )

        def quantize_h(g):
            h_mx[g] = codes_and_scales("h%d" % g, G, tag={0: "w2_raw", 1: "w2_grouped", 3: "w2_raw"}.get(g))
            quantize(h_mx[g], 0, G, hidden[:, 4 * G * g : 4 * G * (g + 1)])

        def second_layer(g):
            quantize_h(g)
            for m in range(2):
                matmul_mx(y_banks[g][:, m, :], w2_mx, slice(P * m, P * (m + 1)), h_mx[g], slice(0, G), True, True)

        def copy_out(copy, g):
            copy(result[:, :, G * g : G * (g + 1)], y_banks[g][:])

        def store(lo, hi):
            nc.sync.dma_start(out_hbm[:, :, G * lo : G * hi], result[:, :, G * lo : G * hi])

        for g in range(GROUPS):
            hide(g)
        nc.vector.tensor_copy(
            w2_grouped[:].rearrange("p (c i j) -> p c j i", i=4, j=4), w2_raw[:].rearrange("p j (c i) -> p c j i", i=4)
        )
        quantize(w2_mx, 0, N, w2_grouped[:])
        for g in range(last):
            second_layer(g)
        copy_out(nc.vector.tensor_copy, 0)
        store(0, 1)
        quantize_h(last)
        copy_out(scalar_copy, 1)
        copy_out(scalar_copy, 2)
        store(1, 3)
        for m, tag in enumerate(("last_bank", "h_bank0")):
            bank = psum.tile([P, G], F32, name="last_bank%d" % m, tag=tag)
            matmul_mx(bank[:], w2_mx, slice(P * m, P * (m + 1)), h_mx[last], slice(0, G), True, True)
            copy = nc.vector.tensor_copy if m == 0 else scalar_copy
            copy(result[:, m, G * last :], bank[:])
        store(last, GROUPS)
